import numpy as np
import ml_dtypes


def mxq(x, axis, fmt="e4m3"):
    dtype, down = {"e4m3": (ml_dtypes.float8_e4m3fn, 7), "e5m2": (ml_dtypes.float8_e5m2, 14)}[fmt]
    v = np.moveaxis(np.asarray(x, np.float32).astype(ml_dtypes.bfloat16).astype(np.float64), axis, -1)
    blocks = v.reshape(v.shape[:-1] + (-1, 32))
    amax = np.abs(blocks).max(-1, keepdims=True)
    byte = np.maximum(np.where(amax > 0, np.frexp(amax)[1] - 1 + 127, 0) - down, 1)
    scale = np.exp2(byte - 127.0)
    codes = (blocks / scale).astype(np.float32).astype(dtype).astype(np.float64)
    return np.moveaxis((codes * scale).reshape(v.shape), -1, axis)


WIDE = False


def mx_kscale(k):
    if not WIDE:
        return np.ones(k)
    levels = np.array([10, -10, 5, -5, 0])
    if k % 512:
        return np.exp2(np.random.permutation(np.resize(levels, k // 32))).repeat(32)
    a = np.empty((k // 512, 16))
    for p in range(k // 512):
        a[p, :8] = np.random.permutation(np.resize(levels, 8))
        for g in range(8):
            far = levels[np.abs(levels - a[p, g]) >= 10]
            a[p, g + 8] = far[np.random.randint(len(far))]
    return np.exp2(a.ravel()).repeat(32)


def f64(x):
    return np.asarray(x).astype(np.float64)


def striped(idx):
    return np.tile(idx.reshape(-1, 16).T, (8, 1)).astype(np.uint16)


def unstriped(offs):
    return offs[:16].T.reshape(-1).astype(np.int64)


K, T, H, N = 1024, 128, 1024, 256


def setup_inputs():
    n = np.random.standard_normal
    s = mx_kscale(K)[:, None]
    u = mx_kscale(H)
    idx = np.random.permutation(H)
    v = np.empty(H)
    v[idx] = u
    return {
        "xT": (n((K, T)) * s).astype(np.float32),
        "w1": (n((K, H)) / np.sqrt(K) / s * v).astype(np.float32),
        "w2": (n((H, N)) / np.sqrt(H) / u[:, None]).astype(np.float32),
        "offs": striped(idx),
    }


def reference(xT, w1, w2, offs):
    idx = unstriped(offs)
    h = mxq(f64(w1), 0, "e4m3").T @ mxq(f64(xT), 0, "e4m3")
    return mxq(f64(w2), 0, "e4m3").T @ mxq(h[idx], 0, "e4m3")

@@ -1,0 +1,166 @@
+import concourse.mybir as mybir
+from concourse.masks import make_identity
+from contextlib import ExitStack
+
+K, T, H, N = 1024, 128, 1024, 256
+FLOPS = 2 * K * H * T + 2 * H * N * T
+
+F32 = mybir.dt.float32
+BF16 = mybir.dt.bfloat16
+U32 = mybir.dt.uint32
+U16 = mybir.dt.uint16
+U8 = mybir.dt.uint8
+FP8X4 = mybir.dt.float8_e4m3fn_x4
+COPY = mybir.ActivationFunctionType.Copy
+MULT = mybir.AluOpType.mult
+ADD = mybir.AluOpType.add
+
+P = 128
+J = 4
+KP = P * J
+
+
+def tile_picked_shuffle_mlp_none_perm_l_kernel(tc, xT, w1, w2, offs, out):
+    nc = tc.nc
+    with ExitStack() as ctx:
+        keep = ctx.enter_context(tc.tile_pool(name="keep", bufs=1))
+        psum = ctx.enter_context(tc.psum_pool(name="psum", bufs=1))
+
+        def sb(shape, dtype, name):
+            return keep.tile(shape, dtype, name=name, align_bytes=64)
+
+        def ps(shape, name):
+            return psum.tile(shape, F32, name=name)
+
+        offsets = keep.tile([P, H // 16], U16, name="offsets")
+        x_raw = sb([P, 2, J, T], F32, "x_raw")
+        nc.sync.dma_start(out=x_raw[:].rearrange("p q j t -> p q (j t)"), in_=xT.rearrange("(q p j) t -> p q (j t)", q=2, j=J))
+
+        pieces = []
+        for q, c0, w, v in ((0, 0, 512, 256), (1, 0, 512, 256), (0, 512, 512, 256), (1, 512, 256, 144), (1, 768, 256, 176)):
+            raw = sb([P, J, w], F32, "w1_raw_%d_%d" % (q, c0))
+            src = w1[q * KP : (q + 1) * KP, c0 : c0 + w].rearrange("(p j) c -> p j c", j=J)
+            nc.sync.dma_start(out=raw[:], in_=src)
+            pieces.append((q, c0, w, v, raw))
+            if len(pieces) == 2:
+                nc.sync.dma_start(offsets[:], offs)
+        w2_raw = []
+        for q in range(2):
+            raw = sb([P, J, N], F32, "w2_raw_%d" % q)
+            nc.sync.dma_start(out=raw[:], in_=w2[q * KP : (q + 1) * KP, :].rearrange("(p j) c -> p j c", j=J))
+            w2_raw.append(raw)
+
+        ident = sb([P, P], F32, "ident")
+        make_identity(nc, ident[:])
+
+        x_grp = sb([P, 2, T, J], BF16, "x_grp")
+        nc.vector.tensor_copy(out=x_grp[:, 0], in_=x_raw[:, 0].rearrange("p j t -> p t j"))
+        nc.scalar.copy(out=x_grp[:, 1], in_=x_raw[:, 1].rearrange("p j t -> p t j"))
+        x_cod = sb([P, 2, T], U32, "x_cod")
+        x_scl = sb([P, 2, T], U8, "x_scl")
+        nc.vector.quantize_mx(
+            out=x_cod[:].rearrange("p q t -> p (q t)").bitcast(FP8X4),
+            scales=x_scl[:].rearrange("p q t -> p (q t)"),
+            in_=x_grp[:].rearrange("p q t j -> p (q t j)"),
+        )
+
+        h32 = sb([P, H], F32, "h32")
+        h16 = sb([P, H], BF16, "h16")
+        banks = {0: ps([P, 512], "h_a"), 512: ps([P, 256], "h_b"), 768: ps([P, 128], "h_c"), 896: ps([P, 128], "h_d")}
+        width = {0: 512, 512: 256, 768: 128, 896: 128}
+
+        def first_layer(q, c0, cod, scl, base):
+            n = width[c0]
+            a = c0 - base
+            nc.tensor.matmul_mx(
+                out=banks[c0][:],
+                lhsT=x_cod[:, q, :].bitcast(FP8X4),
+                lhsT_scale=x_scl[:, q, :],
+                rhs=cod[:, a : a + n].bitcast(FP8X4),
+                rhs_scale=scl[:, a : a + n],
+                start=(q == 0),
+                stop=(q == 1),
+            )
+
+        def to_window(engine, c0):
+            n = width[c0]
+            if engine == "v":
+                nc.vector.tensor_copy(out=h32[:, c0 : c0 + n], in_=banks[c0][:])
+            else:
+                nc.scalar.copy(out=h16[:, c0 : c0 + n], in_=banks[c0][:])
+
+        for q, c0, w, v, raw in pieces:
+            grp = sb([P, w, J], BF16, "w1_grp_%d_%d" % (q, c0))
+            cod = sb([P, w], U32, "w1_cod_%d_%d" % (q, c0))
+            scl = sb([P, w], U8, "w1_scl_%d_%d" % (q, c0))
+            nc.scalar.copy(out=grp[:, v:w], in_=raw[:, :, v:w].rearrange("p j c -> p c j"))
+            nc.vector.tensor_copy(out=grp[:, 0:v], in_=raw[:, :, 0:v].rearrange("p j c -> p c j"))
+            nc.vector.quantize_mx(out=cod[:].bitcast(FP8X4), scales=scl[:], in_=grp[:].rearrange("p c j -> p (c j)"))
+            for b in sorted(banks):
+                if c0 <= b and b < c0 + w:
+                    first_layer(q, b, cod, scl, c0)
+            if q == 1 and c0 < 768:
+                to_window("v", c0)
+                to_window("s", c0)
+        to_window("v", 768)
+        to_window("s", 896)
+        to_window("v", 896)
+        to_window("s", 768)
+
+        picked = []
+        for q in range(2):
+            g = sb([P, KP], BF16, "picked_%d" % q)
+            view = g[:].rearrange("t (u p e) -> t p u e", u=2, e=2)
+            nc.vector.tensor_copy(out=view[:, 0:64], in_=h32[:].indirect(offsets[:, 32 * q : 32 * q + 16]))
+            nc.scalar.activation(out=view[:, 64:128], in_=h16[:].indirect(offsets[:, 32 * q + 16 : 32 * q + 32]), func=COPY)
+            picked.append(g)
+
+        w2_cod = []
+        w2_scl = []
+        for q in range(2):
+            grp = sb([P, N, J], BF16, "w2_grp_%d" % q)
+            nc.gpsimd.tensor_scalar(out=grp[:], in0=w2_raw[q][:].rearrange("p j c -> p c j"), scalar1=1.0, scalar2=0.0, op0=MULT, op1=ADD)
+            cod = sb([P, N], U32, "w2_cod_%d" % q)
+            scl = sb([P, N], U8, "w2_scl_%d" % q)
+            nc.vector.quantize_mx(out=cod[:].bitcast(FP8X4), scales=scl[:], in_=grp[:].rearrange("p c j -> p (c j)"))
+            w2_cod.append(cod)
+            w2_scl.append(scl)
+
+        hg_cod = []
+        hg_scl = []
+        for q in range(2):
+            turned = ps([P, 2, T], "turned_%d" % q)
+            words = picked[q][:].bitcast(F32)
+            for u in range(2):
+                nc.tensor.transpose(turned[:, u, :], words[:, 128 * u : 128 * (u + 1)], ident[:])
+            grp = sb([P, T * J], BF16, "hg_grp_%d" % q)
+            dst = grp[:].bitcast(F32).rearrange("p (t u) -> p t u", u=2)
+            src = turned[:].rearrange("p u t -> p t u")
+            if q == 0:
+                nc.vector.tensor_copy(out=dst, in_=src)
+            else:
+                nc.scalar.copy(out=dst, in_=src)
+            cod = sb([P, T], U32, "hg_cod_%d" % q)
+            scl = sb([P, T], U8, "hg_scl_%d" % q)
+            nc.vector.quantize_mx(out=cod[:].bitcast(FP8X4), scales=scl[:], in_=grp[:])
+            hg_cod.append(cod)
+            hg_scl.append(scl)
+
+        accs = [ps([P, T], "acc_%d" % m) for m in range(2)]
+        for q in range(2):
+            for m in range(2):
+                nc.tensor.matmul_mx(
+                    out=accs[m][:],
+                    lhsT=w2_cod[q][:, 128 * m : 128 * (m + 1)].bitcast(FP8X4),
+                    lhsT_scale=w2_scl[q][:, 128 * m : 128 * (m + 1)],
+                    rhs=hg_cod[q][:].bitcast(FP8X4),
+                    rhs_scale=hg_scl[q][:],
+                    start=(q == 0),
+                    stop=(q == 1),
+                )
+        res0 = sb([P, T], F32, "res0")
+        res1 = sb([P, T], F32, "res1")
+        nc.vector.tensor_copy(out=res0[:], in_=accs[0][:])
+        nc.sync.dma_start(out=out[0:128, :], in_=res0[:])
+        nc.scalar.copy(out=res1[:], in_=accs[1][:])
+        nc.scalar.dma_start(out=out[128:256, :], in_=res1[:])

@@ -29,20 +29,18 @@ def tile_picked_shuffle_mlp_none_perm_l_kernel(tc, xT, w1, w2, offs, out):
         def sb(shape, dtype, name):
             return keep.tile(shape, dtype, name=name, align_bytes=64)
 
-        def ps(shape, name):
-            return psum.tile(shape, F32, name=name)
+        def ps(shape, name, tag):
+            return psum.tile(shape, F32, name=name, tag=tag)
 
         offsets = keep.tile([P, H // 16], U16, name="offsets")
         x_raw = sb([P, 2, J, T], F32, "x_raw")
         nc.sync.dma_start(out=x_raw[:].rearrange("p q j t -> p q (j t)"), in_=xT.rearrange("(q p j) t -> p q (j t)", q=2, j=J))
-
-        pieces = []
-        for q, c0, w, v in ((0, 0, 512, 256), (1, 0, 512, 256), (0, 512, 512, 256), (1, 512, 256, 144), (1, 768, 256, 176)):
+        raws = {}
+        for q, c0, w in ((0, 0, 512), (1, 0, 512), (0, 512, 512), (1, 512, 256), (1, 768, 256)):
             raw = sb([P, J, w], F32, "w1_raw_%d_%d" % (q, c0))
-            src = w1[q * KP : (q + 1) * KP, c0 : c0 + w].rearrange("(p j) c -> p j c", j=J)
-            nc.sync.dma_start(out=raw[:], in_=src)
-            pieces.append((q, c0, w, v, raw))
-            if len(pieces) == 2:
+            nc.sync.dma_start(out=raw[:], in_=w1[q * KP : (q + 1) * KP, c0 : c0 + w].rearrange("(p j) c -> p j c", j=J))
+            raws[q, c0] = raw
+            if len(raws) == 2:
                 nc.sync.dma_start(offsets[:], offs)
         w2_raw = []
         for q in range(2):
@@ -66,46 +64,92 @@ def tile_picked_shuffle_mlp_none_perm_l_kernel(tc, xT, w1, w2, offs, out):
 
         h32 = sb([P, H], F32, "h32")
         h16 = sb([P, H], BF16, "h16")
-        banks = {0: ps([P, 512], "h_a"), 512: ps([P, 256], "h_b"), 768: ps([P, 128], "h_c"), 896: ps([P, 128], "h_d")}
-        width = {0: 512, 512: 256, 768: 128, 896: 128}
+        width = {0: 256, 256: 256, 512: 256, 768: 128, 896: 128}
+        banks = {}
+        for b in sorted(width):
+            banks[b] = ps([P, width[b]], "h_%d" % b, "bank_%d" % b)
 
-        def first_layer(q, c0, cod, scl, base):
-            n = width[c0]
-            a = c0 - base
-            nc.tensor.matmul_mx(
-                out=banks[c0][:],
-                lhsT=x_cod[:, q, :].bitcast(FP8X4),
-                lhsT_scale=x_scl[:, q, :],
-                rhs=cod[:, a : a + n].bitcast(FP8X4),
-                rhs_scale=scl[:, a : a + n],
-                start=(q == 0),
-                stop=(q == 1),
-            )
+        grps = {}
+        for q in range(2):
+            for b in range(0, H, 256):
+                grps[q, b] = sb([P, 256, J], BF16, "w1_grp_%d_%d" % (q, b))
 
-        def to_window(engine, c0):
-            n = width[c0]
+        def interleave(engine, q, raw0, b, lo, hi):
+            dst = grps[q, b][:, lo:hi].rearrange("p (b i) j -> p b j i", i=4)
+            src = raws[q, raw0][:, :, b - raw0 + lo : b - raw0 + hi].rearrange("p j (b i) -> p b j i", i=4)
             if engine == "v":
-                nc.vector.tensor_copy(out=h32[:, c0 : c0 + n], in_=banks[c0][:])
+                nc.vector.tensor_copy(out=dst, in_=src)
             else:
-                nc.scalar.copy(out=h16[:, c0 : c0 + n], in_=banks[c0][:])
+                nc.scalar.copy(out=dst, in_=src)
 
-        for q, c0, w, v, raw in pieces:
-            grp = sb([P, w, J], BF16, "w1_grp_%d_%d" % (q, c0))
-            cod = sb([P, w], U32, "w1_cod_%d_%d" % (q, c0))
-            scl = sb([P, w], U8, "w1_scl_%d_%d" % (q, c0))
-            nc.scalar.copy(out=grp[:, v:w], in_=raw[:, :, v:w].rearrange("p j c -> p c j"))
-            nc.vector.tensor_copy(out=grp[:, 0:v], in_=raw[:, :, 0:v].rearrange("p j c -> p c j"))
-            nc.vector.quantize_mx(out=cod[:].bitcast(FP8X4), scales=scl[:], in_=grp[:].rearrange("p c j -> p (c j)"))
-            for b in sorted(banks):
-                if c0 <= b and b < c0 + w:
-                    first_layer(q, b, cod, scl, c0)
-            if q == 1 and c0 < 768:
-                to_window("v", c0)
-                to_window("s", c0)
-        to_window("v", 768)
-        to_window("s", 896)
-        to_window("v", 896)
-        to_window("s", 768)
+        def quantise(q, b):
+            cod = sb([P, 256], U32, "w1_cod_%d_%d" % (q, b))
+            scl = sb([P, 256], U8, "w1_scl_%d_%d" % (q, b))
+            nc.vector.quantize_mx(out=cod[:].bitcast(FP8X4), scales=scl[:], in_=grps[q, b][:].rearrange("p c j -> p (c j)"))
+            for c in sorted(width):
+                if b <= c and c < b + 256:
+                    a = c - b
+                    n = width[c]
+                    nc.tensor.matmul_mx(
+                        out=banks[c][:],
+                        lhsT=x_cod[:, q, :].bitcast(FP8X4),
+                        lhsT_scale=x_scl[:, q, :],
+                        rhs=cod[:, a : a + n].bitcast(FP8X4),
+                        rhs_scale=scl[:, a : a + n],
+                        start=(q == 0),
+                        stop=(q == 1),
+                    )
+
+        def window32(b, engine="v"):
+            if engine == "v":
+                nc.vector.tensor_copy(out=h32[:, b : b + width[b]], in_=banks[b][:])
+            else:
+                nc.scalar.copy(out=h32[:, b : b + width[b]], in_=banks[b][:])
+
+        def window16(b):
+            nc.scalar.copy(out=h16[:, b : b + width[b]], in_=banks[b][:])
+
+        def pair(q, b, v):
+            interleave("v", q, b, b, 0, 256)
+            interleave("s", q, b, b + 256, v, 256)
+            interleave("v", q, b, b + 256, 0, v)
+
+        pair(0, 0, 88)
+        quantise(0, 0)
+        quantise(0, 256)
+        pair(1, 0, 88)
+        quantise(1, 0)
+        quantise(1, 256)
+        pair(0, 512, 88)
+        window32(0, 's')
+        window16(0)
+        window32(256, 's')
+        window16(256)
+        quantise(0, 512)
+        quantise(0, 768)
+        interleave("v", 1, 512, 512, 0, 256)
+        quantise(1, 512)
+        window32(512, 's')
+        window16(512)
+        interleave("v", 1, 768, 768, 0, 256)
+        quantise(1, 768)
+        window32(768)
+        window16(896)
+        window32(896)
+        window16(768)
+
+        w2_grp = []
+        w2_cod = []
+        w2_scl = []
+        for q in range(2):
+            grp = sb([P, N, J], BF16, "w2_grp_%d" % q)
+            if q == 0:
+                nc.gpsimd.tensor_scalar(out=grp[:], in0=w2_raw[q][:].rearrange("p j c -> p c j"), scalar1=1.0, scalar2=0.0, op0=MULT, op1=ADD)
+            w2_grp.append(grp)
+            cod = sb([P, N], U32, "w2_cod_%d" % q)
+            scl = sb([P, N], U8, "w2_scl_%d" % q)
+            w2_cod.append(cod)
+            w2_scl.append(scl)
 
         picked = []
         for q in range(2):
@@ -115,38 +159,29 @@ def tile_picked_shuffle_mlp_none_perm_l_kernel(tc, xT, w1, w2, offs, out):
             nc.scalar.activation(out=view[:, 64:128], in_=h16[:].indirect(offsets[:, 32 * q + 16 : 32 * q + 32]), func=COPY)
             picked.append(g)
 
-        w2_cod = []
-        w2_scl = []
-        for q in range(2):
-            grp = sb([P, N, J], BF16, "w2_grp_%d" % q)
-            nc.gpsimd.tensor_scalar(out=grp[:], in0=w2_raw[q][:].rearrange("p j c -> p c j"), scalar1=1.0, scalar2=0.0, op0=MULT, op1=ADD)
-            cod = sb([P, N], U32, "w2_cod_%d" % q)
-            scl = sb([P, N], U8, "w2_scl_%d" % q)
-            nc.vector.quantize_mx(out=cod[:].bitcast(FP8X4), scales=scl[:], in_=grp[:].rearrange("p c j -> p (c j)"))
-            w2_cod.append(cod)
-            w2_scl.append(scl)
+        nc.vector.tensor_copy(out=w2_grp[1][:].rearrange("p (b i) j -> p b j i", i=4), in_=w2_raw[1][:].rearrange("p j (b i) -> p b j i", i=4))
 
+        hg_grp = []
         hg_cod = []
         hg_scl = []
         for q in range(2):
-            turned = ps([P, 2, T], "turned_%d" % q)
+            turned = ps([P, 2, T], "turned_%d" % q, "turned_%d" % q)
             words = picked[q][:].bitcast(F32)
             for u in range(2):
                 nc.tensor.transpose(turned[:, u, :], words[:, 128 * u : 128 * (u + 1)], ident[:])
             grp = sb([P, T * J], BF16, "hg_grp_%d" % q)
-            dst = grp[:].bitcast(F32).rearrange("p (t u) -> p t u", u=2)
-            src = turned[:].rearrange("p u t -> p t u")
-            if q == 0:
-                nc.vector.tensor_copy(out=dst, in_=src)
-            else:
-                nc.scalar.copy(out=dst, in_=src)
+            nc.scalar.copy(out=grp[:].bitcast(F32).rearrange("p (t u) -> p t u", u=2), in_=turned[:].rearrange("p u t -> p t u"))
+            hg_grp.append(grp)
             cod = sb([P, T], U32, "hg_cod_%d" % q)
             scl = sb([P, T], U8, "hg_scl_%d" % q)
-            nc.vector.quantize_mx(out=cod[:].bitcast(FP8X4), scales=scl[:], in_=grp[:])
             hg_cod.append(cod)
             hg_scl.append(scl)
 
-        accs = [ps([P, T], "acc_%d" % m) for m in range(2)]
+        for q in range(2):
+            nc.vector.quantize_mx(out=w2_cod[q][:].bitcast(FP8X4), scales=w2_scl[q][:], in_=w2_grp[q][:].rearrange("p c j -> p (c j)"))
+            nc.vector.quantize_mx(out=hg_cod[q][:].bitcast(FP8X4), scales=hg_scl[q][:], in_=hg_grp[q][:])
+
+        accs = [ps([P, T], "acc_%d" % m, "bank_%d" % (256 * m)) for m in range(2)]
         for q in range(2):
             for m in range(2):
                 nc.tensor.matmul_mx(

@@ -36,7 +36,7 @@ def tile_picked_shuffle_mlp_none_perm_l_kernel(tc, xT, w1, w2, offs, out):
         x_raw = sb([P, 2, J, T], F32, "x_raw")
         nc.sync.dma_start(out=x_raw[:].rearrange("p q j t -> p q (j t)"), in_=xT.rearrange("(q p j) t -> p q (j t)", q=2, j=J))
         raws = {}
-        for q, c0, w in ((0, 0, 512), (1, 0, 512), (0, 512, 512), (1, 512, 256), (1, 768, 256)):
+        for q, c0, w in ((0, 0, 1024), (1, 0, 512), (1, 512, 256), (1, 768, 256)):
             raw = sb([P, J, w], F32, "w1_raw_%d_%d" % (q, c0))
             nc.sync.dma_start(out=raw[:], in_=w1[q * KP : (q + 1) * KP, c0 : c0 + w].rearrange("(p j) c -> p j c", j=J))
             raws[q, c0] = raw
@@ -70,9 +70,8 @@ def tile_picked_shuffle_mlp_none_perm_l_kernel(tc, xT, w1, w2, offs, out):
             banks[b] = ps([P, width[b]], "h_%d" % b, "bank_%d" % b)
 
         grps = {}
-        for q in range(2):
-            for b in range(0, H, 256):
-                grps[q, b] = sb([P, 256, J], BF16, "w1_grp_%d_%d" % (q, b))
+        for q, b, n in ((0, 0, 512), (0, 512, 512), (1, 0, 512), (1, 512, 256), (1, 768, 256)):
+            grps[q, b] = sb([P, n, J], BF16, "w1_grp_%d_%d" % (q, b))
 
         def interleave(engine, q, raw0, b, lo, hi):
             dst = grps[q, b][:, lo:hi].rearrange("p (b i) j -> p b j i", i=4)
@@ -82,20 +81,20 @@ def tile_picked_shuffle_mlp_none_perm_l_kernel(tc, xT, w1, w2, offs, out):
             else:
                 nc.scalar.copy(out=dst, in_=src)
 
-        def quantise(q, b):
-            cod = sb([P, 256], U32, "w1_cod_%d_%d" % (q, b))
-            scl = sb([P, 256], U8, "w1_scl_%d_%d" % (q, b))
-            nc.vector.quantize_mx(out=cod[:].bitcast(FP8X4), scales=scl[:], in_=grps[q, b][:].rearrange("p c j -> p (c j)"))
+        def quantise(q, b, lo, hi):
+            n = hi - lo
+            cod = sb([P, n], U32, "w1_cod_%d_%d" % (q, b + lo))
+            scl = sb([P, n], U8, "w1_scl_%d_%d" % (q, b + lo))
+            nc.vector.quantize_mx(out=cod[:].bitcast(FP8X4), scales=scl[:], in_=grps[q, b][:, lo:hi].rearrange("p c j -> p (c j)"))
             for c in sorted(width):
-                if b <= c and c < b + 256:
-                    a = c - b
-                    n = width[c]
+                if b + lo <= c and c < b + hi:
+                    a = c - b - lo
                     nc.tensor.matmul_mx(
                         out=banks[c][:],
                         lhsT=x_cod[:, q, :].bitcast(FP8X4),
                         lhsT_scale=x_scl[:, q, :],
-                        rhs=cod[:, a : a + n].bitcast(FP8X4),
-                        rhs_scale=scl[:, a : a + n],
+                        rhs=cod[:, a : a + width[c]].bitcast(FP8X4),
+                        rhs_scale=scl[:, a : a + width[c]],
                         start=(q == 0),
                         stop=(q == 1),
                     )
@@ -109,30 +108,29 @@ def tile_picked_shuffle_mlp_none_perm_l_kernel(tc, xT, w1, w2, offs, out):
         def window16(b):
             nc.scalar.copy(out=h16[:, b : b + width[b]], in_=banks[b][:])
 
-        def pair(q, b, v):
-            interleave("v", q, b, b, 0, 256)
-            interleave("s", q, b, b + 256, v, 256)
-            interleave("v", q, b, b + 256, 0, v)
-
-        pair(0, 0, 88)
-        quantise(0, 0)
-        quantise(0, 256)
-        pair(1, 0, 88)
-        quantise(1, 0)
-        quantise(1, 256)
-        pair(0, 512, 88)
+        interleave("s", 0, 0, 0, 344, 512)
+        interleave("v", 0, 0, 0, 0, 344)
+        interleave("s", 0, 0, 512, 344, 512)
+        interleave("v", 0, 0, 512, 0, 344)
+        quantise(0, 0, 0, 512)
+        quantise(0, 512, 0, 512)
+        interleave("s", 1, 0, 0, 344, 512)
+        interleave("v", 1, 0, 0, 0, 256)
+        interleave("v", 1, 0, 0, 256, 344)
+        quantise(1, 0, 0, 256)
+        quantise(1, 0, 256, 512)
         window32(0, 's')
         window16(0)
         window32(256, 's')
         window16(256)
-        quantise(0, 512)
-        quantise(0, 768)
         interleave("v", 1, 512, 512, 0, 256)
-        quantise(1, 512)
+        quantise(1, 512, 0, 256)
         window32(512, 's')
         window16(512)
-        interleave("v", 1, 768, 768, 0, 256)
-        quantise(1, 768)
+        interleave("v", 1, 768, 768, 0, 128)
+        interleave("v", 1, 768, 768, 128, 256)
+        quantise(1, 768, 0, 128)
+        quantise(1, 768, 128, 256)
         window32(768)
         window16(896)
         window32(896)

@@ -34,12 +34,14 @@ def tile_picked_shuffle_mlp_none_perm_l_kernel(tc, xT, w1, w2, offs, out):
 
         offsets = keep.tile([P, H // 16], U16, name="offsets")
         x_raw = sb([P, 2, J, T], F32, "x_raw")
-        nc.sync.dma_start(out=x_raw[:].rearrange("p q j t -> p q (j t)"), in_=xT.rearrange("(q p j) t -> p q (j t)", q=2, j=J))
         raws = {}
-        for q, c0, w in ((0, 0, 1024), (1, 0, 512), (1, 512, 256), (1, 768, 256)):
-            raw = sb([P, J, w], F32, "w1_raw_%d_%d" % (q, c0))
-            nc.sync.dma_start(out=raw[:], in_=w1[q * KP : (q + 1) * KP, c0 : c0 + w].rearrange("(p j) c -> p j c", j=J))
-            raws[q, c0] = raw
+        for q, j0, j1, c0, c1 in ((0, 0, 4, 0, 1024), (1, 0, 2, 0, 1024), (1, 2, 4, 0, 512), (1, 2, 4, 512, 768), (1, 2, 4, 768, 1024)):
+            raw = sb([P, j1 - j0, c1 - c0], F32, "w1_raw_%d_%d_%d" % (q, j0, c0))
+            src = w1[q * KP : (q + 1) * KP, :].rearrange("(p j) c -> p j c", j=J)
+            nc.sync.dma_start(out=raw[:], in_=src[:, j0:j1, c0:c1])
+            raws[q, j0, c0] = raw
+            if len(raws) == 1:
+                nc.sync.dma_start(out=x_raw[:].rearrange("p q j t -> p q (j t)"), in_=xT.rearrange("(q p j) t -> p q (j t)", q=2, j=J))
             if len(raws) == 2:
                 nc.sync.dma_start(offsets[:], offs)
         w2_raw = []
@@ -52,15 +54,8 @@ def tile_picked_shuffle_mlp_none_perm_l_kernel(tc, xT, w1, w2, offs, out):
         make_identity(nc, ident[:])
 
         x_grp = sb([P, 2, T, J], BF16, "x_grp")
-        nc.vector.tensor_copy(out=x_grp[:, 0], in_=x_raw[:, 0].rearrange("p j t -> p t j"))
-        nc.scalar.copy(out=x_grp[:, 1], in_=x_raw[:, 1].rearrange("p j t -> p t j"))
         x_cod = sb([P, 2, T], U32, "x_cod")
         x_scl = sb([P, 2, T], U8, "x_scl")
-        nc.vector.quantize_mx(
-            out=x_cod[:].rearrange("p q t -> p (q t)").bitcast(FP8X4),
-            scales=x_scl[:].rearrange("p q t -> p (q t)"),
-            in_=x_grp[:].rearrange("p q t j -> p (q t j)"),
-        )
 
         h32 = sb([P, H], F32, "h32")
         h16 = sb([P, H], BF16, "h16")
@@ -69,26 +64,44 @@ def tile_picked_shuffle_mlp_none_perm_l_kernel(tc, xT, w1, w2, offs, out):
         for b in sorted(width):
             banks[b] = ps([P, width[b]], "h_%d" % b, "bank_%d" % b)
 
-        grps = {}
-        for q, b, n in ((0, 0, 512), (0, 512, 512), (1, 0, 512), (1, 512, 256), (1, 768, 256)):
-            grps[q, b] = sb([P, n, J], BF16, "w1_grp_%d_%d" % (q, b))
+        grps = [sb([P, H, J], BF16, "w1_grp_%d" % q) for q in range(2)]
 
-        def interleave(engine, q, raw0, b, lo, hi):
-            dst = grps[q, b][:, lo:hi].rearrange("p (b i) j -> p b j i", i=4)
-            src = raws[q, raw0][:, :, b - raw0 + lo : b - raw0 + hi].rearrange("p j (b i) -> p b j i", i=4)
+        def interleave(engine, q, j0, j1, c0, lo, hi):
+            dst = grps[q][:, lo:hi, j0:j1]
+            src = raws[q, j0, c0][:, :, lo - c0 : hi - c0]
+            if j1 - j0 == J:
+                dst = dst.rearrange("p (b i) j -> p b j i", i=4)
+                src = src.rearrange("p j (b i) -> p b j i", i=4)
+            else:
+                src = src.rearrange("p j c -> p c j")
             if engine == "v":
                 nc.vector.tensor_copy(out=dst, in_=src)
             else:
                 nc.scalar.copy(out=dst, in_=src)
 
-        def quantise(q, b, lo, hi):
+        def interleave_x(engine, q):
+            dst = x_grp[:, q].rearrange("p (b i) j -> p b j i", i=4)
+            src = x_raw[:, q].rearrange("p j (b i) -> p b j i", i=4)
+            if engine == "v":
+                nc.vector.tensor_copy(out=dst, in_=src)
+            else:
+                nc.scalar.copy(out=dst, in_=src)
+
+        def quantise_x():
+            nc.vector.quantize_mx(
+                out=x_cod[:].rearrange("p q t -> p (q t)").bitcast(FP8X4),
+                scales=x_scl[:].rearrange("p q t -> p (q t)"),
+                in_=x_grp[:].rearrange("p q t j -> p (q t j)"),
+            )
+
+        def quantise(q, lo, hi):
             n = hi - lo
-            cod = sb([P, n], U32, "w1_cod_%d_%d" % (q, b + lo))
-            scl = sb([P, n], U8, "w1_scl_%d_%d" % (q, b + lo))
-            nc.vector.quantize_mx(out=cod[:].bitcast(FP8X4), scales=scl[:], in_=grps[q, b][:, lo:hi].rearrange("p c j -> p (c j)"))
+            cod = sb([P, n], U32, "w1_cod_%d_%d" % (q, lo))
+            scl = sb([P, n], U8, "w1_scl_%d_%d" % (q, lo))
+            nc.vector.quantize_mx(out=cod[:].bitcast(FP8X4), scales=scl[:], in_=grps[q][:, lo:hi].rearrange("p c j -> p (c j)"))
             for c in sorted(width):
-                if b + lo <= c and c < b + hi:
-                    a = c - b - lo
+                if lo <= c and c < hi:
+                    a = c - lo
                     nc.tensor.matmul_mx(
                         out=banks[c][:],
                         lhsT=x_cod[:, q, :].bitcast(FP8X4),
@@ -108,29 +121,35 @@ def tile_picked_shuffle_mlp_none_perm_l_kernel(tc, xT, w1, w2, offs, out):
         def window16(b):
             nc.scalar.copy(out=h16[:, b : b + width[b]], in_=banks[b][:])
 
-        interleave("s", 0, 0, 0, 344, 512)
-        interleave("v", 0, 0, 0, 0, 344)
-        interleave("s", 0, 0, 512, 344, 512)
-        interleave("v", 0, 0, 512, 0, 344)
-        quantise(0, 0, 0, 512)
-        quantise(0, 512, 0, 512)
-        interleave("s", 1, 0, 0, 344, 512)
-        interleave("v", 1, 0, 0, 0, 256)
-        interleave("v", 1, 0, 0, 256, 344)
-        quantise(1, 0, 0, 256)
-        quantise(1, 0, 256, 512)
+        interleave("s", 0, 0, 4, 0, 344, 512)
+        interleave("v", 0, 0, 4, 0, 0, 344)
+        interleave("s", 0, 0, 4, 0, 856, 1024)
+        interleave("v", 0, 0, 4, 0, 512, 856)
+        interleave_x("s", 0)
+        interleave_x("s", 1)
+        quantise_x()
+        quantise(0, 0, 512)
+        quantise(0, 512, 1024)
+        interleave("s", 1, 0, 2, 0, 640, 1024)
+        interleave("v", 1, 0, 2, 0, 0, 640)
+        interleave("s", 1, 2, 4, 0, 344, 512)
+        interleave("v", 1, 2, 4, 0, 0, 256)
+        interleave("v", 1, 2, 4, 0, 256, 344)
+        quantise(1, 0, 256)
+        quantise(1, 256, 512)
+        interleave("s", 1, 2, 4, 512, 688, 768)
+        interleave("v", 1, 2, 4, 512, 512, 688)
         window32(0, 's')
         window16(0)
         window32(256, 's')
         window16(256)
-        interleave("v", 1, 512, 512, 0, 256)
-        quantise(1, 512, 0, 256)
-        window32(512, 's')
+        quantise(1, 512, 768)
+        interleave("v", 1, 2, 4, 768, 768, 896)
+        interleave("v", 1, 2, 4, 768, 896, 1024)
+        quantise(1, 768, 896)
+        quantise(1, 896, 1024)
+        window32(512)
         window16(512)
-        interleave("v", 1, 768, 768, 0, 128)
-        interleave("v", 1, 768, 768, 128, 256)
-        quantise(1, 768, 0, 128)
-        quantise(1, 768, 128, 256)
         window32(768)
         window16(896)
         window32(896)
@@ -140,9 +159,11 @@ def tile_picked_shuffle_mlp_none_perm_l_kernel(tc, xT, w1, w2, offs, out):
         w2_cod = []
         w2_scl = []
         for q in range(2):
-            grp = sb([P, N, J], BF16, "w2_grp_%d" % q)
+            grp = grps[1][:, 768 - 256 * q : 1024 - 256 * q]
             if q == 0:
-                nc.gpsimd.tensor_scalar(out=grp[:], in0=w2_raw[q][:].rearrange("p j c -> p c j"), scalar1=1.0, scalar2=0.0, op0=MULT, op1=ADD)
+                nc.gpsimd.tensor_scalar(out=grp, in0=w2_raw[q][:].rearrange("p j c -> p c j"), scalar1=1.0, scalar2=0.0, op0=MULT, op1=ADD)
+            else:
+                nc.gpsimd.tensor_scalar(out=grp[:, 128:], in0=w2_raw[q][:, :, 128:].rearrange("p j c -> p c j"), scalar1=1.0, scalar2=0.0, op0=MULT, op1=ADD)
             w2_grp.append(grp)
             cod = sb([P, N], U32, "w2_cod_%d" % q)
             scl = sb([P, N], U8, "w2_scl_%d" % q)
@@ -156,8 +177,6 @@ def tile_picked_shuffle_mlp_none_perm_l_kernel(tc, xT, w1, w2, offs, out):
             nc.vector.tensor_copy(out=view[:, 0:64], in_=h32[:].indirect(offsets[:, 32 * q : 32 * q + 16]))
             nc.scalar.activation(out=view[:, 64:128], in_=h16[:].indirect(offsets[:, 32 * q + 16 : 32 * q + 32]), func=COPY)
             picked.append(g)
-
-        nc.vector.tensor_copy(out=w2_grp[1][:].rearrange("p (b i) j -> p b j i", i=4), in_=w2_raw[1][:].rearrange("p j (b i) -> p b j i", i=4))
 
         hg_grp = []
         hg_cod = []
@@ -175,9 +194,13 @@ def tile_picked_shuffle_mlp_none_perm_l_kernel(tc, xT, w1, w2, offs, out):
             hg_cod.append(cod)
             hg_scl.append(scl)
 
-        for q in range(2):
-            nc.vector.quantize_mx(out=w2_cod[q][:].bitcast(FP8X4), scales=w2_scl[q][:], in_=w2_grp[q][:].rearrange("p c j -> p (c j)"))
-            nc.vector.quantize_mx(out=hg_cod[q][:].bitcast(FP8X4), scales=hg_scl[q][:], in_=hg_grp[q][:])
+        nc.vector.quantize_mx(out=w2_cod[0][:].bitcast(FP8X4), scales=w2_scl[0][:], in_=w2_grp[0].rearrange("p c j -> p (c j)"))
+        nc.vector.quantize_mx(out=hg_cod[0][:].bitcast(FP8X4), scales=hg_scl[0][:], in_=hg_grp[0][:])
+        late = hg_grp[0][:].rearrange("p (c j) -> p c j", j=J)
+        nc.vector.tensor_copy(out=late.rearrange("p (b i) j -> p b j i", i=4), in_=w2_raw[1][:, :, 0:128].rearrange("p j (b i) -> p b j i", i=4))
+        nc.vector.quantize_mx(out=w2_cod[1][:, 128:256].bitcast(FP8X4), scales=w2_scl[1][:, 128:256], in_=w2_grp[1][:, 128:256].rearrange("p c j -> p (c j)"))
+        nc.vector.quantize_mx(out=w2_cod[1][:, 0:128].bitcast(FP8X4), scales=w2_scl[1][:, 0:128], in_=hg_grp[0][:])
+        nc.vector.quantize_mx(out=hg_cod[1][:].bitcast(FP8X4), scales=hg_scl[1][:], in_=hg_grp[1][:])
 
         accs = [ps([P, T], "acc_%d" % m, "bank_%d" % (256 * m)) for m in range(2)]
         for q in range(2):

import concourse.mybir as mybir
from concourse.masks import make_identity
from contextlib import ExitStack

K, T, H, N = 1024, 128, 1024, 256
FLOPS = 2 * K * H * T + 2 * H * N * T

F32 = mybir.dt.float32
BF16 = mybir.dt.bfloat16
U32 = mybir.dt.uint32
U16 = mybir.dt.uint16
U8 = mybir.dt.uint8
FP8X4 = mybir.dt.float8_e4m3fn_x4
COPY = mybir.ActivationFunctionType.Copy
MULT = mybir.AluOpType.mult
ADD = mybir.AluOpType.add

P = 128
J = 4
KP = P * J


def tile_picked_shuffle_mlp_none_perm_l_kernel(tc, xT, w1, w2, offs, out):
    nc = tc.nc
    with ExitStack() as ctx:
        keep = ctx.enter_context(tc.tile_pool(name="keep", bufs=1))
        psum = ctx.enter_context(tc.psum_pool(name="psum", bufs=1))

        def sb(shape, dtype, name):
            return keep.tile(shape, dtype, name=name, align_bytes=64)

        def ps(shape, name, tag):
            return psum.tile(shape, F32, name=name, tag=tag)

        offsets = keep.tile([P, H // 16], U16, name="offsets")
        x_raw = sb([P, 2, J, T], F32, "x_raw")
        raws = {}
        for q, j0, j1, c0, c1 in ((0, 0, 4, 0, 1024), (1, 0, 2, 0, 1024), (1, 2, 4, 0, 512), (1, 2, 4, 512, 768), (1, 2, 4, 768, 1024)):
            raw = sb([P, j1 - j0, c1 - c0], F32, "w1_raw_%d_%d_%d" % (q, j0, c0))
            src = w1[q * KP : (q + 1) * KP, :].rearrange("(p j) c -> p j c", j=J)
            nc.sync.dma_start(out=raw[:], in_=src[:, j0:j1, c0:c1])
            raws[q, j0, c0] = raw
            if len(raws) == 1:
                nc.sync.dma_start(out=x_raw[:].rearrange("p q j t -> p q (j t)"), in_=xT.rearrange("(q p j) t -> p q (j t)", q=2, j=J))
            if len(raws) == 2:
                nc.sync.dma_start(offsets[:], offs)
        w2_raw = []
        for q in range(2):
            raw = sb([P, J, N], F32, "w2_raw_%d" % q)
            nc.sync.dma_start(out=raw[:], in_=w2[q * KP : (q + 1) * KP, :].rearrange("(p j) c -> p j c", j=J))
            w2_raw.append(raw)

        ident = sb([P, P], F32, "ident")
        make_identity(nc, ident[:])

        x_grp = sb([P, 2, T, J], BF16, "x_grp")
        x_cod = sb([P, 2, T], U32, "x_cod")
        x_scl = sb([P, 2, T], U8, "x_scl")

        h32 = sb([P, H], F32, "h32")
        h16 = sb([P, H], BF16, "h16")
        width = {0: 256, 256: 256, 512: 256, 768: 128, 896: 128}
        banks = {}
        for b in sorted(width):
            banks[b] = ps([P, width[b]], "h_%d" % b, "bank_%d" % b)

        grps = [sb([P, H, J], BF16, "w1_grp_%d" % q) for q in range(2)]

        def interleave(engine, q, j0, j1, c0, lo, hi):
            dst = grps[q][:, lo:hi, j0:j1]
            src = raws[q, j0, c0][:, :, lo - c0 : hi - c0]
            if j1 - j0 == J:
                dst = dst.rearrange("p (b i) j -> p b j i", i=4)
                src = src.rearrange("p j (b i) -> p b j i", i=4)
            else:
                src = src.rearrange("p j c -> p c j")
            if engine == "v":
                nc.vector.tensor_copy(out=dst, in_=src)
            else:
                nc.scalar.copy(out=dst, in_=src)

        def interleave_x(engine, q):
            dst = x_grp[:, q].rearrange("p (b i) j -> p b j i", i=4)
            src = x_raw[:, q].rearrange("p j (b i) -> p b j i", i=4)
            if engine == "v":
                nc.vector.tensor_copy(out=dst, in_=src)
            else:
                nc.scalar.copy(out=dst, in_=src)

        def quantise_x():
            nc.vector.quantize_mx(
                out=x_cod[:].rearrange("p q t -> p (q t)").bitcast(FP8X4),
                scales=x_scl[:].rearrange("p q t -> p (q t)"),
                in_=x_grp[:].rearrange("p q t j -> p (q t j)"),
            )

        def quantise(q, lo, hi):
            n = hi - lo
            cod = sb([P, n], U32, "w1_cod_%d_%d" % (q, lo))
            scl = sb([P, n], U8, "w1_scl_%d_%d" % (q, lo))
            nc.vector.quantize_mx(out=cod[:].bitcast(FP8X4), scales=scl[:], in_=grps[q][:, lo:hi].rearrange("p c j -> p (c j)"))
            for c in sorted(width):
                if lo <= c and c < hi:
                    a = c - lo
                    nc.tensor.matmul_mx(
                        out=banks[c][:],
                        lhsT=x_cod[:, q, :].bitcast(FP8X4),
                        lhsT_scale=x_scl[:, q, :],
                        rhs=cod[:, a : a + width[c]].bitcast(FP8X4),
                        rhs_scale=scl[:, a : a + width[c]],
                        start=(q == 0),
                        stop=(q == 1),
                    )

        def window32(b, engine="v"):
            if engine == "v":
                nc.vector.tensor_copy(out=h32[:, b : b + width[b]], in_=banks[b][:])
            else:
                nc.scalar.copy(out=h32[:, b : b + width[b]], in_=banks[b][:])

        def window16(b):
            nc.scalar.copy(out=h16[:, b : b + width[b]], in_=banks[b][:])

        interleave("s", 0, 0, 4, 0, 344, 512)
        interleave("v", 0, 0, 4, 0, 0, 344)
        interleave("s", 0, 0, 4, 0, 856, 1024)
        interleave("v", 0, 0, 4, 0, 512, 856)
        interleave_x("s", 0)
        interleave_x("s", 1)
        quantise_x()
        quantise(0, 0, 512)
        quantise(0, 512, 1024)
        interleave("s", 1, 0, 2, 0, 640, 1024)
        interleave("v", 1, 0, 2, 0, 0, 640)
        interleave("s", 1, 2, 4, 0, 344, 512)
        interleave("v", 1, 2, 4, 0, 0, 256)
        interleave("v", 1, 2, 4, 0, 256, 344)
        quantise(1, 0, 256)
        quantise(1, 256, 512)
        interleave("s", 1, 2, 4, 512, 688, 768)
        interleave("v", 1, 2, 4, 512, 512, 688)
        window32(0, 's')
        window16(0)
        window32(256, 's')
        window16(256)
        quantise(1, 512, 768)
        interleave("v", 1, 2, 4, 768, 768, 896)
        interleave("v", 1, 2, 4, 768, 896, 1024)
        quantise(1, 768, 896)
        quantise(1, 896, 1024)
        window32(512)
        window16(512)
        window32(768)
        window16(896)
        window32(896)
        window16(768)

        w2_grp = []
        w2_cod = []
        w2_scl = []
        for q in range(2):
            grp = grps[1][:, 768 - 256 * q : 1024 - 256 * q]
            if q == 0:
                nc.gpsimd.tensor_scalar(out=grp, in0=w2_raw[q][:].rearrange("p j c -> p c j"), scalar1=1.0, scalar2=0.0, op0=MULT, op1=ADD)
            else:
                nc.gpsimd.tensor_scalar(out=grp[:, 128:], in0=w2_raw[q][:, :, 128:].rearrange("p j c -> p c j"), scalar1=1.0, scalar2=0.0, op0=MULT, op1=ADD)
            w2_grp.append(grp)
            cod = sb([P, N], U32, "w2_cod_%d" % q)
            scl = sb([P, N], U8, "w2_scl_%d" % q)
            w2_cod.append(cod)
            w2_scl.append(scl)

        picked = []
        for q in range(2):
            g = sb([P, KP], BF16, "picked_%d" % q)
            view = g[:].rearrange("t (u p e) -> t p u e", u=2, e=2)
            nc.vector.tensor_copy(out=view[:, 0:64], in_=h32[:].indirect(offsets[:, 32 * q : 32 * q + 16]))
            nc.scalar.activation(out=view[:, 64:128], in_=h16[:].indirect(offsets[:, 32 * q + 16 : 32 * q + 32]), func=COPY)
            picked.append(g)

        hg_grp = []
        hg_cod = []
        hg_scl = []
        for q in range(2):
            turned = ps([P, 2, T], "turned_%d" % q, "turned_%d" % q)
            words = picked[q][:].bitcast(F32)
            for u in range(2):
                nc.tensor.transpose(turned[:, u, :], words[:, 128 * u : 128 * (u + 1)], ident[:])
            grp = sb([P, T * J], BF16, "hg_grp_%d" % q)
            nc.scalar.copy(out=grp[:].bitcast(F32).rearrange("p (t u) -> p t u", u=2), in_=turned[:].rearrange("p u t -> p t u"))
            hg_grp.append(grp)
            cod = sb([P, T], U32, "hg_cod_%d" % q)
            scl = sb([P, T], U8, "hg_scl_%d" % q)
            hg_cod.append(cod)
            hg_scl.append(scl)

        nc.vector.quantize_mx(out=w2_cod[0][:].bitcast(FP8X4), scales=w2_scl[0][:], in_=w2_grp[0].rearrange("p c j -> p (c j)"))
        nc.vector.quantize_mx(out=hg_cod[0][:].bitcast(FP8X4), scales=hg_scl[0][:], in_=hg_grp[0][:])
        late = hg_grp[0][:].rearrange("p (c j) -> p c j", j=J)
        nc.vector.tensor_copy(out=late.rearrange("p (b i) j -> p b j i", i=4), in_=w2_raw[1][:, :, 0:128].rearrange("p j (b i) -> p b j i", i=4))
        nc.vector.quantize_mx(out=w2_cod[1][:, 128:256].bitcast(FP8X4), scales=w2_scl[1][:, 128:256], in_=w2_grp[1][:, 128:256].rearrange("p c j -> p (c j)"))
        nc.vector.quantize_mx(out=w2_cod[1][:, 0:128].bitcast(FP8X4), scales=w2_scl[1][:, 0:128], in_=hg_grp[0][:])
        nc.vector.quantize_mx(out=hg_cod[1][:].bitcast(FP8X4), scales=hg_scl[1][:], in_=hg_grp[1][:])

        accs = [ps([P, T], "acc_%d" % m, "bank_%d" % (256 * m)) for m in range(2)]
        for q in range(2):
            for m in range(2):
                nc.tensor.matmul_mx(
                    out=accs[m][:],
                    lhsT=w2_cod[q][:, 128 * m : 128 * (m + 1)].bitcast(FP8X4),
                    lhsT_scale=w2_scl[q][:, 128 * m : 128 * (m + 1)],
                    rhs=hg_cod[q][:].bitcast(FP8X4),
                    rhs_scale=hg_scl[q][:],
                    start=(q == 0),
                    stop=(q == 1),
                )
        res0 = sb([P, T], F32, "res0")
        res1 = sb([P, T], F32, "res1")
        nc.vector.tensor_copy(out=res0[:], in_=accs[0][:])
        nc.sync.dma_start(out=out[0:128, :], in_=res0[:])
        nc.scalar.copy(out=res1[:], in_=accs[1][:])
        nc.scalar.dma_start(out=out[128:256, :], in_=res1[:])
